import numpy as np
import ml_dtypes


def mxq(x, axis, fmt="e4m3"):
    dtype, down = {"e4m3": (ml_dtypes.float8_e4m3fn, 7), "e5m2": (ml_dtypes.float8_e5m2, 14)}[fmt]
    v = np.moveaxis(np.asarray(x, np.float32).astype(ml_dtypes.bfloat16).astype(np.float64), axis, -1)
    blocks = v.reshape(v.shape[:-1] + (-1, 32))
    amax = np.abs(blocks).max(-1, keepdims=True)
    byte = np.maximum(np.where(amax > 0, np.frexp(amax)[1] - 1 + 127, 0) - down, 1)
    scale = np.exp2(byte - 127.0)
    codes = (blocks / scale).astype(np.float32).astype(dtype).astype(np.float64)
    return np.moveaxis((codes * scale).reshape(v.shape), -1, axis)


WIDE = False


def mx_kscale(k, group=512):
    if not WIDE:
        return np.ones(k)
    levels = np.array([10, -10, 5, -5, 0])
    if group != 512:
        return np.exp2(np.random.permutation(np.resize(levels, k // group))).repeat(group)
    if k % 512:
        return np.exp2(np.random.permutation(np.resize(levels, k // 32))).repeat(32)
    a = np.empty((k // 512, 16))
    for p in range(k // 512):
        a[p, :8] = np.random.permutation(np.resize(levels, 8))
        for g in range(8):
            far = levels[np.abs(levels - a[p, g]) >= 10]
            a[p, g + 8] = far[np.random.randint(len(far))]
    return np.exp2(a.ravel()).repeat(32)


def f64(x):
    return np.asarray(x).astype(np.float64)


def striped(idx):
    return np.tile(np.asarray(idx).reshape(-1, 16).T, (8, 1)).astype(np.uint16)


def unstriped(offs):
    return offs[:16].T.reshape(-1).astype(np.int64)


H, KV, D, NQ, N = 8, 8, 128, 512, 512


def setup_inputs():
    n = np.random.standard_normal
    s = mx_kscale(D, 0)[:, None]
    u = mx_kscale(N)
    t = np.random.uniform(0.5, 2.0, N) * u
    v = n((KV, N, 128))
    v[:, :, 127] = 1.0
    return {
        "qT": (n((H, D, NQ)) * s * (0.70 / np.sqrt(D))).astype(np.float32),
        "kT": (n((KV, D, N)) / s).astype(np.float32),
        "t": t.reshape(N, 1).astype(np.float32),
        "v": (v / t[:, None]).astype(np.float32),
        "kb": (0.5 * n((N, 1))).astype(np.float32),
        "mask": (np.arange(N)[:, None] <= np.sort(np.random.randint(N // 4, N, NQ))[None, :]).astype(np.float32),
        "og": n((H, NQ, 128)).astype(np.float32),
    }


def reference(qT, kT, t, v, kb, mask, og):
    a = mxq(f64(kT), 1, "e4m3").transpose(0, 2, 1) @ mxq(f64(qT), 1, "e4m3")
    a = a + f64(kb)
    p = np.exp(a)
    p = p * f64(mask)
    w = p * f64(t)
    y = mxq(w, 1, "e4m3").transpose(0, 2, 1) @ mxq(f64(v), 1, "e4m3")
    y = y / (y[:, :, 127:128])
    y = y / (1.0 + np.exp(-f64(og)))
    return y

@@ -1,0 +1,362 @@
+from contextlib import ExitStack
+
+import concourse.mybir as mybir
+
+H, D, NQ, N = 8, 128, 512, 512
+FLOPS = 2 * 2 * H * NQ * N * D
+
+F32 = mybir.dt.float32
+BF16 = mybir.dt.bfloat16
+U32 = mybir.dt.uint32
+U8 = mybir.dt.uint8
+FP8X4 = mybir.dt.float8_e4m3fn_x4
+ACT = mybir.ActivationFunctionType
+ALU = mybir.AluOpType
+
+P = 128
+PACK = 4
+ROWS = D // PACK
+G = P // ROWS
+SETS = H // G
+QT = 128
+NQT = NQ // QT
+UNITS = SETS * NQT
+DEPTH = 3
+
+
+def tile_rows_a_exp_kb_mask_gate_kernel(tc, qT, kT, t, v, kb, mask, og, out):
+    nc = tc.nc
+    with ExitStack() as ctx:
+        sb = ctx.enter_context(tc.tile_pool(name="sb", bufs=1))
+        ps = ctx.enter_context(tc.psum_pool(name="ps", bufs=1))
+        ctx.enter_context(tc.manual_schedule())
+
+        def tiles(name, count, shape, dtype):
+            return [sb.tile(shape, dtype, name="%s%d" % (name, i), align_bytes=64) for i in range(count)]
+
+        k_raw = tiles("k_raw", SETS * 2, [P, PACK, N // 2], F32)
+        q_raw = tiles("q_raw", UNITS, [P, PACK, QT], F32)
+        v_raw = tiles("v_raw", SETS * 2, [P, 2, PACK, D], F32)
+        og_raw = tiles("og_raw", UNITS, [P, G, D], F32)
+        mask_raw = tiles("mask_raw", NQT, [P, PACK, QT], F32)
+        kb_raw = sb.tile([P, PACK], F32, name="kb_raw")
+        t_raw = sb.tile([P, PACK], F32, name="t_raw")
+        kb_exp = sb.tile([P, PACK], F32, name="kb_exp")
+        token_factor = sb.tile([P, PACK], F32, name="token_factor")
+        half_col = sb.tile([P, 1], F32, name="half_col")
+        factor = tiles("factor", NQT, [P, QT * PACK], F32)
+        k_bf = tiles("k_bf", SETS * 2, [P, PACK, N // 2], BF16)
+        q_bf = tiles("q_bf", UNITS, [P, QT * PACK], BF16)
+        v_bf = tiles("v_bf", SETS * 2, [P, 2 * D * PACK], BF16)
+        k_codes = tiles("k_codes", SETS, [P, N], U32)
+        k_scales = tiles("k_scales", SETS, [P, N], U8)
+        q_codes = tiles("q_codes", UNITS, [P, QT], U32)
+        q_scales = tiles("q_scales", UNITS, [P, QT], U8)
+        v_codes = tiles("v_codes", SETS, [P, G * D], U32)
+        v_scales = tiles("v_scales", SETS, [P, G * D], U8)
+        p_exp = tiles("p_exp", DEPTH, [P, G, QT * PACK], F32)
+        w_bf = tiles("w_bf", 2, [P, G * QT * PACK], BF16)
+        w_codes = tiles("w_codes", 4, [P, G * QT], U32)
+        w_scales = tiles("w_scales", 4, [P, G * QT], U8)
+        th = tiles("th", UNITS, [P, G, D], F32)
+        gate = tiles("gate", 4, [P, G, D], F32)
+        inv = tiles("inv", 4, [P, G], F32)
+        res = tiles("res", UNITS, [P, G, D], F32)
+        score = [ps.tile([P, PACK, QT], F32, name="score%d" % g) for g in range(G)]
+        y_acc = [ps.tile([P, G, D], F32, name="y_acc%d" % i) for i in range(4)]
+
+        def heads(s):
+            return slice(s * G, (s + 1) * G)
+
+        def qcols(u):
+            c = u % NQT
+            return slice(c * QT, (c + 1) * QT)
+
+        def load_q(u):
+            src = qT[heads(u // NQT)].rearrange("h (p j) n -> (h p) j n", j=PACK)
+            nc.sync.dma_start(out=q_raw[u][:], in_=src[:, :, qcols(u)])
+
+        def load_k(s, half):
+            src = kT[heads(s)].rearrange("h (p j) n -> (h p) j n", j=PACK)
+            nc.sync.dma_start(out=k_raw[2 * s + half][:], in_=src[:, :, half * 256 : (half + 1) * 256])
+
+        def load_v(s, half):
+            h0 = s * G + 2 * half
+            nc.sync.dma_start(
+                out=v_raw[2 * s + half][:].rearrange("p h j e -> p h (j e)"),
+                in_=v[h0 : h0 + 2].rearrange("h (p j) e -> p h (j e)", j=PACK),
+            )
+
+        def load_mask(c):
+            nc.sync.dma_start(out=mask_raw[c][:], in_=mask.rearrange("(p j) n -> p j n", j=PACK)[:, :, qcols(c)])
+
+        def load_og(u):
+            nc.sync.dma_start(out=og_raw[u][:], in_=og[heads(u // NQT), qcols(u), :].rearrange("h p e -> p h e"))
+
+        def copy(engine, dst, src):
+            if engine is nc.vector:
+                nc.vector.tensor_copy(out=dst, in_=src)
+            else:
+                nc.scalar.copy(out=dst, in_=src)
+
+        def cast_q(u, engine):
+            copy(
+                engine,
+                q_bf[u][:].rearrange("p (c i j) -> p c j i", i=4, j=PACK),
+                q_raw[u][:].rearrange("p j (c i) -> p c j i", i=4),
+            )
+
+        def cast_k(s, half, engine):
+            copy(
+                engine,
+                k_bf[2 * s + half][:].rearrange("p r (s j) -> p s j r", j=PACK),
+                k_raw[2 * s + half][:].rearrange("p j (s r) -> p s j r", r=PACK),
+            )
+
+        def cast_v(s, half, engine):
+            copy(
+                engine,
+                v_bf[2 * s + half][:].rearrange("p (h c i j) -> p h c j i", h=2, i=4, j=PACK),
+                v_raw[2 * s + half][:].rearrange("p h j (c i) -> p h c j i", i=4),
+            )
+
+        def quantize(codes, scales, src):
+            nc.vector.quantize_mx(out=codes.bitcast(FP8X4), scales=scales, in_=src)
+
+        def quant_q(u):
+            quantize(q_codes[u][:], q_scales[u][:], q_bf[u][:])
+
+        def quant_k(s, half):
+            for r in range(PACK):
+                cols = slice(r * P + half * 64, r * P + (half + 1) * 64)
+                quantize(k_codes[s][:, cols], k_scales[s][:, cols], k_bf[2 * s + half][:, r, :])
+
+        def quant_v(s, half):
+            cols = slice(half * 2 * D, (half + 1) * 2 * D)
+            quantize(v_codes[s][:, cols], v_scales[s][:, cols], v_bf[2 * s + half][:])
+
+        def make_factor(c):
+            nc.vector.tensor_tensor(
+                out=factor[c][:].rearrange("p (n j) -> p n j", j=PACK),
+                in0=mask_raw[c][:].rearrange("p j n -> p n j"),
+                in1=token_factor[:].unsqueeze(1).to_broadcast([P, QT, PACK]),
+                op=ALU.mult,
+            )
+
+        def scores(u):
+            s = u // NQT
+            for g in range(G):
+                rows = slice(g * ROWS, (g + 1) * ROWS)
+                for r in range(PACK):
+                    cols = slice(r * P, (r + 1) * P)
+                    nc.tensor.matmul_mx(
+                        out=score[g][:, r, :],
+                        lhsT=k_codes[s][rows, cols].bitcast(FP8X4),
+                        lhsT_scale=k_scales[s][rows, cols],
+                        rhs=q_codes[u][rows, :].bitcast(FP8X4),
+                        rhs_scale=q_scales[u][rows, :],
+                        start=True,
+                        stop=True,
+                    )
+
+        def exps(u):
+            for g in range(G):
+                nc.scalar.activation(
+                    out=p_exp[u % DEPTH][:, g, :].rearrange("p (n r) -> p n r", r=PACK),
+                    in_=score[g][:].rearrange("p r n -> p n r"),
+                    func=ACT.Exp,
+                )
+
+        def weigh(u, g0, g1):
+            width = QT * PACK
+            nc.vector.tensor_tensor(
+                out=w_bf[u % 2][:, g0 * width : g1 * width].rearrange("p (g n) -> p g n", n=width),
+                in0=p_exp[u % DEPTH][:, g0:g1, :],
+                in1=factor[u % NQT][:].unsqueeze(1).to_broadcast([P, g1 - g0, width]),
+                op=ALU.mult,
+            )
+
+        def quant_w(u, g0, g1):
+            quantize(
+                w_codes[u % 4][:, g0 * QT : g1 * QT],
+                w_scales[u % 4][:, g0 * QT : g1 * QT],
+                w_bf[u % 2][:, g0 * QT * PACK : g1 * QT * PACK],
+            )
+
+        def values(u, g0, g1):
+            s = u // NQT
+            for g in range(g0, g1):
+                cols = slice(g * QT, (g + 1) * QT)
+                nc.tensor.matmul_mx(
+                    out=y_acc[u % 4][:, g, :],
+                    lhsT=w_codes[u % 4][:, cols].bitcast(FP8X4),
+                    lhsT_scale=w_scales[u % 4][:, cols],
+                    rhs=v_codes[s][:, g * D : (g + 1) * D].bitcast(FP8X4),
+                    rhs_scale=v_scales[s][:, g * D : (g + 1) * D],
+                    start=True,
+                    stop=True,
+                )
+
+        def tanh_gate(u):
+            nc.scalar.activation(out=th[u][:], in_=og_raw[u][:], func=ACT.Tanh, scale=0.5)
+
+        def invert(u):
+            nc.vector.reciprocal(out=inv[u % 4][:], in_=y_acc[u % 4][:, :, D - 1])
+
+        def make_gate(u):
+            for g in range(G):
+                col = inv[u % 4][:, g : g + 1]
+                nc.vector.tensor_scalar(
+                    out=gate[u % 4][:, g, :], in0=th[u][:, g, :],
+                    scalar1=col, scalar2=col, op0=ALU.mult, op1=ALU.add,
+                )
+
+        def sigmoid_gate(u):
+            nc.scalar.activation(out=gate[u % 4][:], in_=th[u][:], func=ACT.Identity, scale=0.5, bias=half_col[:])
+
+        def invert_part(u, g0, g1):
+            nc.vector.reciprocal(out=inv[u % 4][:, g0:g1], in_=y_acc[u % 4][:, g0:g1, D - 1])
+
+        def finish_part(u, g0, g1):
+            for g in range(g0, g1):
+                nc.vector.scalar_tensor_tensor(
+                    out=res[u][:, g, :],
+                    in0=y_acc[u % 4][:, g, :],
+                    scalar=inv[u % 4][:, g : g + 1],
+                    in1=gate[u % 4][:, g, :],
+                    op0=ALU.mult,
+                    op1=ALU.mult,
+                )
+            h0 = (u // NQT) * G
+            nc.sync.dma_start(
+                out=out[h0 + g0 : h0 + g1, qcols(u), :].rearrange("h p e -> p h e"), in_=res[u][:, g0:g1, :]
+            )
+
+        def finish(u):
+            nc.vector.scalar_tensor_tensor(
+                out=res[u][:].rearrange("p g e -> p (g e)"),
+                in0=y_acc[u % 4][:].rearrange("p g e -> p (g e)"),
+                scalar=0.5,
+                in1=gate[u % 4][:].rearrange("p g e -> p (g e)"),
+                op0=ALU.mult,
+                op1=ALU.mult,
+            )
+            nc.sync.dma_start(out=out[heads(u // NQT), qcols(u), :].rearrange("h p e -> p h e"), in_=res[u][:])
+
+        nc.scalar.dma_start(out=kb_raw[:], in_=kb.rearrange("(p j) o -> p (j o)", j=PACK))
+        nc.scalar.dma_start(out=t_raw[:], in_=t.rearrange("(p j) o -> p (j o)", j=PACK))
+        load_k(0, 0)
+        load_k(0, 1)
+        load_q(0)
+        load_mask(0)
+        load_q(1)
+        load_mask(1)
+        load_q(2)
+        load_v(0, 0)
+        load_v(0, 1)
+        load_mask(2)
+        load_q(3)
+        load_og(0)
+        load_k(1, 0)
+        load_k(1, 1)
+        load_mask(3)
+        load_q(4)
+        load_og(1)
+        load_q(5)
+        load_og(2)
+        load_v(1, 0)
+        load_v(1, 1)
+        load_q(6)
+        load_og(3)
+        load_q(7)
+        load_og(4)
+        load_og(5)
+        load_og(6)
+        load_og(7)
+
+        S, V = nc.scalar, nc.vector
+        nc.gpsimd.memset(half_col[:], 0.5)
+        nc.scalar.activation(out=kb_exp[:], in_=kb_raw[:], func=ACT.Exp)
+        nc.vector.tensor_tensor(out=token_factor[:], in0=kb_exp[:], in1=t_raw[:], op=ALU.mult)
+        cast_k(0, 0, V)
+        quant_k(0, 0)
+        cast_k(0, 1, V)
+        cast_q(0, S)
+        quant_k(0, 1)
+        quant_q(0)
+        cast_q(1, S)
+        make_factor(0)
+        scores(0)
+        exps(0)
+        quant_q(1)
+        make_factor(1)
+
+        scalar_extra = {
+            0: [lambda: cast_q(3, S), lambda: cast_k(1, 0, S)],
+            1: [lambda: cast_k(1, 1, S), lambda: cast_q(4, S)],
+            2: [lambda: tanh_gate(0), lambda: cast_q(5, S)],
+            3: [lambda: tanh_gate(1), lambda: cast_q(6, S), lambda: cast_v(1, 0, S)],
+            4: [lambda: tanh_gate(2), lambda: cast_q(7, S), lambda: cast_v(1, 1, S)],
+            5: [lambda: tanh_gate(3), lambda: tanh_gate(4)],
+            6: [lambda: sigmoid_gate(4), lambda: tanh_gate(5), lambda: sigmoid_gate(5), lambda: tanh_gate(6),
+                lambda: sigmoid_gate(6), lambda: tanh_gate(7)],
+        }
+        vector_extra = {
+            1: [lambda: cast_v(0, 1, V), lambda: quant_q(3), lambda: make_factor(2), lambda: quant_k(1, 0), lambda: quant_v(0, 1)],
+            2: [lambda: quant_k(1, 1), lambda: quant_q(4), lambda: make_factor(3)],
+            3: [lambda: quant_q(5)],
+            4: [lambda: quant_q(6), lambda: quant_v(1, 0)],
+            5: [lambda: quant_q(7), lambda: quant_v(1, 1)],
+        }
+        last = UNITS - 1
+        LAG = 3
+        for u in range(UNITS - 1):
+            scores(u + 1)
+            if u >= LAG - 1:
+                values(u - LAG + 1, 0, G)
+            exps(u + 1)
+            for job in scalar_extra.get(u, []):
+                job()
+            if u == 0:
+                weigh(0, 0, 1)
+                cast_q(2, V)
+                weigh(0, 1, 2)
+                quant_q(2)
+                weigh(0, 2, 3)
+                weigh(0, 3, 4)
+                cast_v(0, 0, V)
+                quant_w(0, 0, G)
+                quant_v(0, 0)
+                continue
+            weigh(u, 0, 2)
+            if u >= LAG:
+                invert(u - LAG)
+            weigh(u, 2, 4)
+            if u >= LAG:
+                make_gate(u - LAG)
+            jobs = vector_extra.get(u, [])
+            for job in jobs[:1]:
+                job()
+            quant_w(u, 0, G)
+            if u >= LAG:
+                finish(u - LAG)
+            for job in jobs[1:]:
+                job()
+        sigmoid_gate(7)
+        values(5, 0, G)
+        invert(4)
+        weigh(last, 0, 2)
+        values(6, 0, G)
+        finish_part(4, 0, 4)
+        quant_w(last, 0, 2)
+        invert(5)
+        weigh(last, 2, 4)
+        values(last, 0, 2)
+        finish_part(5, 0, 4)
+        quant_w(last, 2, 4)
+        invert(6)
+        values(last, 2, 4)
+        finish_part(6, 0, 4)
+        invert(last)
+        finish_part(last, 0, 2)
+        finish_part(last, 2, 4)

@@ -22,10 +22,12 @@ QT = 128
 NQT = NQ // QT
 UNITS = SETS * NQT
 DEPTH = 3
+K_SPLIT = 88
 
 
 def tile_rows_a_exp_kb_mask_gate_kernel(tc, qT, kT, t, v, kb, mask, og, out):
     nc = tc.nc
+    S, V = nc.scalar, nc.vector
     with ExitStack() as ctx:
         sb = ctx.enter_context(tc.tile_pool(name="sb", bufs=1))
         ps = ctx.enter_context(tc.psum_pool(name="ps", bufs=1))
@@ -34,117 +36,125 @@ def tile_rows_a_exp_kb_mask_gate_kernel(tc, qT, kT, t, v, kb, mask, og, out):
         def tiles(name, count, shape, dtype):
             return [sb.tile(shape, dtype, name="%s%d" % (name, i), align_bytes=64) for i in range(count)]
 
-        k_raw = tiles("k_raw", SETS * 2, [P, PACK, N // 2], F32)
-        q_raw = tiles("q_raw", UNITS, [P, PACK, QT], F32)
-        v_raw = tiles("v_raw", SETS * 2, [P, 2, PACK, D], F32)
-        og_raw = tiles("og_raw", UNITS, [P, G, D], F32)
-        mask_raw = tiles("mask_raw", NQT, [P, PACK, QT], F32)
+        k_raw = tiles("k_raw", SETS, [P, PACK, N], F32)
+        q_first = sb.tile([P, PACK, QT], F32, name="q_first")
+        q_rest = sb.tile([P, PACK, NQ - QT], F32, name="q_rest")
+        q_late = sb.tile([P, PACK, NQ], F32, name="q_late")
+        v_raw = tiles("v_raw", SETS, [P, G, PACK, D], F32)
+        og_raw = tiles("og_raw", NQT, [P, G, D], F32)
+        og_late = sb.tile([P, G, NQT * D], F32, name="og_late")
+        mask_first = sb.tile([P, PACK, QT], F32, name="mask_first")
+        mask_rest = sb.tile([P, PACK, NQ - QT], F32, name="mask_rest")
+        scaled_first = sb.tile([P, PACK, QT], F32, name="scaled_first")
+        scaled_rest = sb.tile([P, PACK, NQ - QT], F32, name="scaled_rest")
         kb_raw = sb.tile([P, PACK], F32, name="kb_raw")
         t_raw = sb.tile([P, PACK], F32, name="t_raw")
         kb_exp = sb.tile([P, PACK], F32, name="kb_exp")
         token_factor = sb.tile([P, PACK], F32, name="token_factor")
-        half_col = sb.tile([P, 1], F32, name="half_col")
-        factor = tiles("factor", NQT, [P, QT * PACK], F32)
-        k_bf = tiles("k_bf", SETS * 2, [P, PACK, N // 2], BF16)
-        q_bf = tiles("q_bf", UNITS, [P, QT * PACK], BF16)
-        v_bf = tiles("v_bf", SETS * 2, [P, 2 * D * PACK], BF16)
+        factor = sb.tile([P, NQ * PACK], F32, name="factor")
+        k_bf = tiles("k_bf", SETS, [P, N * PACK], BF16)
+        q_bf = tiles("q_bf", SETS, [P, NQ * PACK], BF16)
+        v_bf = tiles("v_bf", SETS, [P, G * D * PACK], BF16)
         k_codes = tiles("k_codes", SETS, [P, N], U32)
         k_scales = tiles("k_scales", SETS, [P, N], U8)
-        q_codes = tiles("q_codes", UNITS, [P, QT], U32)
-        q_scales = tiles("q_scales", UNITS, [P, QT], U8)
+        q_codes = tiles("q_codes", SETS, [P, NQ], U32)
+        q_scales = tiles("q_scales", SETS, [P, NQ], U8)
         v_codes = tiles("v_codes", SETS, [P, G * D], U32)
         v_scales = tiles("v_scales", SETS, [P, G * D], U8)
         p_exp = tiles("p_exp", DEPTH, [P, G, QT * PACK], F32)
         w_bf = tiles("w_bf", 2, [P, G * QT * PACK], BF16)
-        w_codes = tiles("w_codes", 4, [P, G * QT], U32)
-        w_scales = tiles("w_scales", 4, [P, G * QT], U8)
-        th = tiles("th", UNITS, [P, G, D], F32)
-        gate = tiles("gate", 4, [P, G, D], F32)
-        inv = tiles("inv", 4, [P, G], F32)
-        res = tiles("res", UNITS, [P, G, D], F32)
+        w_codes = tiles("w_codes", UNITS, [P, G * QT], U32)
+        w_scales = tiles("w_scales", UNITS, [P, G * QT], U8)
+        th = tiles("th", NQT, [P, 4, D], F32)
+        gate = tiles("gate", 2, [P, 4, D], F32)
+        late_gate = tiles("late_gate", G, [P, 4, D], F32)
+        inv = tiles("inv", UNITS, [P, 4], F32)
+        res = tiles("res", UNITS, [P, 4, D], F32)
         score = [ps.tile([P, PACK, QT], F32, name="score%d" % g) for g in range(G)]
-        y_acc = [ps.tile([P, G, D], F32, name="y_acc%d" % i) for i in range(4)]
+        y_acc = [ps.tile([P, 4, D], F32, name="y_acc%d" % i) for i in range(4)]
 
         def heads(s):
             return slice(s * G, (s + 1) * G)
 
-        def qcols(u):
-            c = u % NQT
-            return slice(c * QT, (c + 1) * QT)
+        def by_feature(x, s):
+            return x[heads(s)].rearrange("h (p j) n -> (h p) j n", j=PACK)
 
-        def load_q(u):
-            src = qT[heads(u // NQT)].rearrange("h (p j) n -> (h p) j n", j=PACK)
-            nc.sync.dma_start(out=q_raw[u][:], in_=src[:, :, qcols(u)])
+        mask_rows = mask.rearrange("(p j) n -> p j n", j=PACK)
 
-        def load_k(s, half):
-            src = kT[heads(s)].rearrange("h (p j) n -> (h p) j n", j=PACK)
-            nc.sync.dma_start(out=k_raw[2 * s + half][:], in_=src[:, :, half * 256 : (half + 1) * 256])
-
-        def load_v(s, half):
-            h0 = s * G + 2 * half
+        def load_v(s):
             nc.sync.dma_start(
-                out=v_raw[2 * s + half][:].rearrange("p h j e -> p h (j e)"),
-                in_=v[h0 : h0 + 2].rearrange("h (p j) e -> p h (j e)", j=PACK),
+                out=v_raw[s][:].rearrange("p h j e -> p h (j e)"),
+                in_=v[heads(s)].rearrange("h (p j) e -> p h (j e)", j=PACK),
             )
 
-        def load_mask(c):
-            nc.sync.dma_start(out=mask_raw[c][:], in_=mask.rearrange("(p j) n -> p j n", j=PACK)[:, :, qcols(c)])
-
-        def load_og(u):
-            nc.sync.dma_start(out=og_raw[u][:], in_=og[heads(u // NQT), qcols(u), :].rearrange("h p e -> p h e"))
+        def load_og(c):
+            nc.sync.dma_start(out=og_raw[c][:], in_=og[heads(0), c * QT : (c + 1) * QT, :].rearrange("h p e -> p h e"))
 
         def copy(engine, dst, src):
-            if engine is nc.vector:
+            if engine is V:
                 nc.vector.tensor_copy(out=dst, in_=src)
             else:
                 nc.scalar.copy(out=dst, in_=src)
 
-        def cast_q(u, engine):
+        def interleave(engine, dst, src):
             copy(
                 engine,
-                q_bf[u][:].rearrange("p (c i j) -> p c j i", i=4, j=PACK),
-                q_raw[u][:].rearrange("p j (c i) -> p c j i", i=4),
+                dst.rearrange("p (c i j) -> p c j i", i=4, j=PACK),
+                src.rearrange("p j (c i) -> p c j i", i=4),
             )
 
-        def cast_k(s, half, engine):
+        def deal(engine, dst, src, lo, hi):
             copy(
                 engine,
-                k_bf[2 * s + half][:].rearrange("p r (s j) -> p s j r", j=PACK),
-                k_raw[2 * s + half][:].rearrange("p j (s r) -> p s j r", r=PACK),
+                dst[:].rearrange("p (r s j) -> p s j r", r=4, j=PACK)[:, lo:hi],
+                src[:].rearrange("p j (s r) -> p s j r", r=4)[:, lo:hi],
             )
+
+        def cast_q0(c0, c1, engine):
+            src = q_first[:] if c0 == 0 else q_rest[:, :, (c0 - 1) * QT : (c1 - 1) * QT]
+            interleave(engine, q_bf[0][:, c0 * QT * PACK : c1 * QT * PACK], src)
+
+        def cast_k1(half, engine):
+            deal(engine, k_bf[1], k_raw[1], half * 64, (half + 1) * 64)
+
+        def cast_q1(half, engine):
+            deal(engine, q_bf[1], q_late, half * 64, (half + 1) * 64)
 
         def cast_v(s, half, engine):
-            copy(
-                engine,
-                v_bf[2 * s + half][:].rearrange("p (h c i j) -> p h c j i", h=2, i=4, j=PACK),
-                v_raw[2 * s + half][:].rearrange("p h j (c i) -> p h c j i", i=4),
+            dst = v_bf[s][:].rearrange("p (h c i j) -> p h c j i", h=G, i=4, j=PACK)
+            src = v_raw[s][:].rearrange("p h j (c i) -> p h c j i", i=4)
+            copy(engine, dst[:, 2 * half : 2 * half + 2], src[:, 2 * half : 2 * half + 2])
+
+        def quantize(codes, scales, src, lo, hi):
+            nc.vector.quantize_mx(
+                out=codes[:, lo:hi].bitcast(FP8X4), scales=scales[:, lo:hi], in_=src[:, lo * PACK : hi * PACK]
             )
 
-        def quantize(codes, scales, src):
-            nc.vector.quantize_mx(out=codes.bitcast(FP8X4), scales=scales, in_=src)
+        def quant_q(s, c0, c1):
+            quantize(q_codes[s], q_scales[s], q_bf[s], c0 * QT, c1 * QT)
 
-        def quant_q(u):
-            quantize(q_codes[u][:], q_scales[u][:], q_bf[u][:])
+        def quant_k(s):
+            quantize(k_codes[s], k_scales[s], k_bf[s], 0, N)
 
-        def quant_k(s, half):
-            for r in range(PACK):
-                cols = slice(r * P + half * 64, r * P + (half + 1) * 64)
-                quantize(k_codes[s][:, cols], k_scales[s][:, cols], k_bf[2 * s + half][:, r, :])
+        def quant_v(s):
+            quantize(v_codes[s], v_scales[s], v_bf[s], 0, G * D)
 
-        def quant_v(s, half):
-            cols = slice(half * 2 * D, (half + 1) * 2 * D)
-            quantize(v_codes[s][:, cols], v_scales[s][:, cols], v_bf[2 * s + half][:])
+        def scale_mask(c0, c1, engine):
+            cols = slice((c0 - 1) * QT, (c1 - 1) * QT)
+            scaled, raw = (scaled_first, mask_first) if c0 == 0 else (scaled_rest[:, :, cols], mask_rest[:, :, cols])
+            for j in range(PACK):
+                col = token_factor[:, j : j + 1]
+                if engine is V:
+                    nc.vector.tensor_scalar(out=scaled[:, j, :], in0=raw[:, j, :], scalar1=col, scalar2=None, op0=ALU.mult)
+                else:
+                    nc.scalar.activation(out=scaled[:, j, :], in_=raw[:, j, :], func=ACT.Copy, scale=col)
 
-        def make_factor(c):
-            nc.vector.tensor_tensor(
-                out=factor[c][:].rearrange("p (n j) -> p n j", j=PACK),
-                in0=mask_raw[c][:].rearrange("p j n -> p n j"),
-                in1=token_factor[:].unsqueeze(1).to_broadcast([P, QT, PACK]),
-                op=ALU.mult,
-            )
+        def make_factor(c0, c1):
+            src = scaled_first[:] if c0 == 0 else scaled_rest[:, :, (c0 - 1) * QT : (c1 - 1) * QT]
+            interleave(V, factor[:, c0 * QT * PACK : c1 * QT * PACK], src)
 
         def scores(u):
-            s = u // NQT
+            s, c = divmod(u, NQT)
             for g in range(G):
                 rows = slice(g * ROWS, (g + 1) * ROWS)
                 for r in range(PACK):
@@ -153,8 +163,8 @@ def tile_rows_a_exp_kb_mask_gate_kernel(tc, qT, kT, t, v, kb, mask, og, out):
                         out=score[g][:, r, :],
                         lhsT=k_codes[s][rows, cols].bitcast(FP8X4),
                         lhsT_scale=k_scales[s][rows, cols],
-                        rhs=q_codes[u][rows, :].bitcast(FP8X4),
-                        rhs_scale=q_scales[u][rows, :],
+                        rhs=q_codes[s][rows, c * QT : (c + 1) * QT].bitcast(FP8X4),
+                        rhs_scale=q_scales[s][rows, c * QT : (c + 1) * QT],
                         start=True,
                         stop=True,
                     )
@@ -168,195 +178,221 @@ def tile_rows_a_exp_kb_mask_gate_kernel(tc, qT, kT, t, v, kb, mask, og, out):
                 )
 
         def weigh(u, g0, g1):
+            s, c = divmod(u, NQT)
             width = QT * PACK
+            if s == 0:
+                unit_factor = factor[:].rearrange("p (c n j) -> p c n j", c=NQT, j=PACK)[:, c]
+            else:
+                unit_factor = factor[:].rearrange("p (n c j) -> p c n j", c=NQT, j=PACK)[:, c]
             nc.vector.tensor_tensor(
-                out=w_bf[u % 2][:, g0 * width : g1 * width].rearrange("p (g n) -> p g n", n=width),
-                in0=p_exp[u % DEPTH][:, g0:g1, :],
-                in1=factor[u % NQT][:].unsqueeze(1).to_broadcast([P, g1 - g0, width]),
+                out=w_bf[u % 2][:, g0 * width : g1 * width].rearrange("p (g n j) -> p g n j", n=QT, j=PACK),
+                in0=p_exp[u % DEPTH][:, g0:g1, :].rearrange("p g (n j) -> p g n j", j=PACK),
+                in1=unit_factor.unsqueeze(1).to_broadcast([P, g1 - g0, QT, PACK]),
                 op=ALU.mult,
             )
 
         def quant_w(u, g0, g1):
-            quantize(
-                w_codes[u % 4][:, g0 * QT : g1 * QT],
-                w_scales[u % 4][:, g0 * QT : g1 * QT],
-                w_bf[u % 2][:, g0 * QT * PACK : g1 * QT * PACK],
+            quantize(w_codes[u], w_scales[u], w_bf[u % 2], g0 * QT, g1 * QT)
+
+        def value(u, g):
+            s, c = divmod(u, NQT)
+            cols = slice(g * QT, (g + 1) * QT)
+            nc.tensor.matmul_mx(
+                out=y_acc[c][:, g, :] if s == 0 else y_acc[g][:, c, :],
+                lhsT=w_codes[u][:, cols].bitcast(FP8X4),
+                lhsT_scale=w_scales[u][:, cols],
+                rhs=v_codes[s][:, g * D : (g + 1) * D].bitcast(FP8X4),
+                rhs_scale=v_scales[s][:, g * D : (g + 1) * D],
+                start=True,
+                stop=True,
             )
 
-        def values(u, g0, g1):
-            s = u // NQT
-            for g in range(g0, g1):
-                cols = slice(g * QT, (g + 1) * QT)
-                nc.tensor.matmul_mx(
-                    out=y_acc[u % 4][:, g, :],
-                    lhsT=w_codes[u % 4][:, cols].bitcast(FP8X4),
-                    lhsT_scale=w_scales[u % 4][:, cols],
-                    rhs=v_codes[s][:, g * D : (g + 1) * D].bitcast(FP8X4),
-                    rhs_scale=v_scales[s][:, g * D : (g + 1) * D],
-                    start=True,
-                    stop=True,
-                )
-
-        def tanh_gate(u):
-            nc.scalar.activation(out=th[u][:], in_=og_raw[u][:], func=ACT.Tanh, scale=0.5)
-
-        def invert(u):
-            nc.vector.reciprocal(out=inv[u % 4][:], in_=y_acc[u % 4][:, :, D - 1])
-
-        def make_gate(u):
+        def values(u):
             for g in range(G):
-                col = inv[u % 4][:, g : g + 1]
+                value(u, g)
+
+        def tanh_gate(c):
+            nc.scalar.activation(out=th[c][:], in_=og_raw[c][:], func=ACT.Tanh, scale=0.5)
+
+        def invert(b):
+            nc.vector.reciprocal(out=inv[b][:], in_=y_acc[b % 4][:, :, D - 1])
+
+        def make_gate(c, engine):
+            for g in range(G):
+                col = inv[c][:, g : g + 1]
+                if engine is S:
+                    nc.scalar.activation(
+                        out=gate[c % 2][:, g, :], in_=th[c][:, g, :], func=ACT.Identity, scale=col, bias=col
+                    )
+                    continue
                 nc.vector.tensor_scalar(
-                    out=gate[u % 4][:, g, :], in0=th[u][:, g, :],
-                    scalar1=col, scalar2=col, op0=ALU.mult, op1=ALU.add,
+                    out=gate[c % 2][:, g, :], in0=th[c][:, g, :], scalar1=col, scalar2=col, op0=ALU.mult, op1=ALU.add
                 )
 
-        def sigmoid_gate(u):
-            nc.scalar.activation(out=gate[u % 4][:], in_=th[u][:], func=ACT.Identity, scale=0.5, bias=half_col[:])
-
-        def invert_part(u, g0, g1):
-            nc.vector.reciprocal(out=inv[u % 4][:, g0:g1], in_=y_acc[u % 4][:, g0:g1, D - 1])
-
-        def finish_part(u, g0, g1):
-            for g in range(g0, g1):
-                nc.vector.scalar_tensor_tensor(
-                    out=res[u][:, g, :],
-                    in0=y_acc[u % 4][:, g, :],
-                    scalar=inv[u % 4][:, g : g + 1],
-                    in1=gate[u % 4][:, g, :],
-                    op0=ALU.mult,
-                    op1=ALU.mult,
-                )
-            h0 = (u // NQT) * G
-            nc.sync.dma_start(
-                out=out[h0 + g0 : h0 + g1, qcols(u), :].rearrange("h p e -> p h e"), in_=res[u][:, g0:g1, :]
-            )
-
-        def finish(u):
+        def finish_early(c):
             nc.vector.scalar_tensor_tensor(
-                out=res[u][:].rearrange("p g e -> p (g e)"),
-                in0=y_acc[u % 4][:].rearrange("p g e -> p (g e)"),
+                out=res[c][:].rearrange("p g e -> p (g e)"),
+                in0=y_acc[c][:].rearrange("p g e -> p (g e)"),
                 scalar=0.5,
-                in1=gate[u % 4][:].rearrange("p g e -> p (g e)"),
+                in1=gate[c % 2][:].rearrange("p g e -> p (g e)"),
                 op0=ALU.mult,
                 op1=ALU.mult,
             )
-            nc.sync.dma_start(out=out[heads(u // NQT), qcols(u), :].rearrange("h p e -> p h e"), in_=res[u][:])
+            nc.sync.dma_start(out=out[heads(0), c * QT : (c + 1) * QT, :].rearrange("h p e -> p h e"), in_=res[c][:])
+
+        def sigmoid_early(c):
+            nc.scalar.activation(out=th[c][:], in_=og_raw[c][:], func=ACT.Sigmoid)
+
+        def finish_mid(c):
+            for g in range(G):
+                nc.vector.scalar_tensor_tensor(
+                    out=res[c][:, g, :],
+                    in0=y_acc[c][:, g, :],
+                    scalar=inv[c][:, g : g + 1],
+                    in1=th[c][:, g, :],
+                    op0=ALU.mult,
+                    op1=ALU.mult,
+                )
+            nc.sync.dma_start(out=out[heads(0), c * QT : (c + 1) * QT, :].rearrange("h p e -> p h e"), in_=res[c][:])
+
+        def sigmoid_gate(g):
+            nc.scalar.activation(out=late_gate[g][:].rearrange("p c e -> p (c e)"), in_=og_late[:, g, :], func=ACT.Sigmoid)
+
+        def finish_late(g, c0, c1):
+            for c in range(c0, c1):
+                nc.vector.scalar_tensor_tensor(
+                    out=res[NQT + g][:, c, :],
+                    in0=y_acc[g][:, c, :],
+                    scalar=inv[NQT + g][:, c : c + 1],
+                    in1=late_gate[g][:, c, :],
+                    op0=ALU.mult,
+                    op1=ALU.mult,
+                )
+            nc.sync.dma_start(
+                out=out[G + g].rearrange("(p c) e -> p c e", c=NQT)[:, c0:c1, :], in_=res[NQT + g][:, c0:c1, :]
+            )
 
         nc.scalar.dma_start(out=kb_raw[:], in_=kb.rearrange("(p j) o -> p (j o)", j=PACK))
         nc.scalar.dma_start(out=t_raw[:], in_=t.rearrange("(p j) o -> p (j o)", j=PACK))
-        load_k(0, 0)
-        load_k(0, 1)
-        load_q(0)
-        load_mask(0)
-        load_q(1)
-        load_mask(1)
-        load_q(2)
-        load_v(0, 0)
-        load_v(0, 1)
-        load_mask(2)
-        load_q(3)
+        nc.sync.dma_start(out=k_raw[0][:], in_=by_feature(kT, 0))
+        nc.sync.dma_start(out=q_first[:], in_=by_feature(qT, 0)[:, :, :QT])
+        nc.sync.dma_start(out=mask_first[:], in_=mask_rows[:, :, :QT])
+        nc.sync.dma_start(out=q_rest[:], in_=by_feature(qT, 0)[:, :, QT:])
+        nc.sync.dma_start(out=mask_rest[:], in_=mask_rows[:, :, QT:])
+        nc.sync.dma_start(out=k_raw[1][:], in_=by_feature(kT, 1))
+        nc.sync.dma_start(out=q_late[:], in_=by_feature(qT, 1))
+        load_v(0)
         load_og(0)
-        load_k(1, 0)
-        load_k(1, 1)
-        load_mask(3)
-        load_q(4)
         load_og(1)
-        load_q(5)
+        load_v(1)
         load_og(2)
-        load_v(1, 0)
-        load_v(1, 1)
-        load_q(6)
         load_og(3)
-        load_q(7)
-        load_og(4)
-        load_og(5)
-        load_og(6)
-        load_og(7)
+        nc.sync.dma_start(out=og_late[:], in_=og[heads(1)].rearrange("h (p c) e -> p h (c e)", c=NQT))
 
-        S, V = nc.scalar, nc.vector
-        nc.gpsimd.memset(half_col[:], 0.5)
         nc.scalar.activation(out=kb_exp[:], in_=kb_raw[:], func=ACT.Exp)
         nc.vector.tensor_tensor(out=token_factor[:], in0=kb_exp[:], in1=t_raw[:], op=ALU.mult)
-        cast_k(0, 0, V)
-        quant_k(0, 0)
-        cast_k(0, 1, V)
-        cast_q(0, S)
-        quant_k(0, 1)
-        quant_q(0)
-        cast_q(1, S)
-        make_factor(0)
+        deal(V, k_bf[0], k_raw[0], 0, K_SPLIT)
+        deal(S, k_bf[0], k_raw[0], K_SPLIT, P)
+        cast_q0(0, 1, S)
+        quant_k(0)
+        quant_q(0, 0, 1)
+        scale_mask(0, 1, V)
         scores(0)
         exps(0)
-        quant_q(1)
-        make_factor(1)
-
-        scalar_extra = {
-            0: [lambda: cast_q(3, S), lambda: cast_k(1, 0, S)],
-            1: [lambda: cast_k(1, 1, S), lambda: cast_q(4, S)],
-            2: [lambda: tanh_gate(0), lambda: cast_q(5, S)],
-            3: [lambda: tanh_gate(1), lambda: cast_q(6, S), lambda: cast_v(1, 0, S)],
-            4: [lambda: tanh_gate(2), lambda: cast_q(7, S), lambda: cast_v(1, 1, S)],
-            5: [lambda: tanh_gate(3), lambda: tanh_gate(4)],
-            6: [lambda: sigmoid_gate(4), lambda: tanh_gate(5), lambda: sigmoid_gate(5), lambda: tanh_gate(6),
-                lambda: sigmoid_gate(6), lambda: tanh_gate(7)],
-        }
-        vector_extra = {
-            1: [lambda: cast_v(0, 1, V), lambda: quant_q(3), lambda: make_factor(2), lambda: quant_k(1, 0), lambda: quant_v(0, 1)],
-            2: [lambda: quant_k(1, 1), lambda: quant_q(4), lambda: make_factor(3)],
-            3: [lambda: quant_q(5)],
-            4: [lambda: quant_q(6), lambda: quant_v(1, 0)],
-            5: [lambda: quant_q(7), lambda: quant_v(1, 1)],
-        }
-        last = UNITS - 1
-        LAG = 3
-        for u in range(UNITS - 1):
-            scores(u + 1)
-            if u >= LAG - 1:
-                values(u - LAG + 1, 0, G)
-            exps(u + 1)
-            for job in scalar_extra.get(u, []):
-                job()
-            if u == 0:
-                weigh(0, 0, 1)
-                cast_q(2, V)
-                weigh(0, 1, 2)
-                quant_q(2)
-                weigh(0, 2, 3)
-                weigh(0, 3, 4)
-                cast_v(0, 0, V)
-                quant_w(0, 0, G)
-                quant_v(0, 0)
-                continue
-            weigh(u, 0, 2)
-            if u >= LAG:
-                invert(u - LAG)
-            weigh(u, 2, 4)
-            if u >= LAG:
-                make_gate(u - LAG)
-            jobs = vector_extra.get(u, [])
-            for job in jobs[:1]:
-                job()
-            quant_w(u, 0, G)
-            if u >= LAG:
-                finish(u - LAG)
-            for job in jobs[1:]:
-                job()
-        sigmoid_gate(7)
-        values(5, 0, G)
+        make_factor(0, 1)
+        cast_q0(1, 2, V)
+        weigh(0, 0, 1)
+        quant_q(0, 1, 2)
+        scores(1)
+        exps(1)
+        cast_k1(0, S)
+        weigh(0, 1, 2)
+        cast_q0(2, 4, V)
+        weigh(0, 2, 3)
+        quant_q(0, 2, 4)
+        scale_mask(1, 4, V)
+        weigh(0, 3, 4)
+        make_factor(1, 4)
+        quant_w(0, 0, G)
+        scores(2)
+        exps(2)
+        cast_k1(1, S)
+        cast_q1(0, S)
+        weigh(1, 0, 2)
+        weigh(1, 2, 4)
+        cast_q1(1, V)
+        quant_w(1, 0, G)
+        scores(3)
+        exps(3)
+        cast_v(0, 0, S)
+        weigh(2, 0, 2)
+        quant_k(1)
+        quant_q(1, 0, 1)
+        weigh(2, 2, 4)
+        quant_q(1, 1, 2)
+        quant_w(2, 0, G)
+        scores(4)
+        exps(4)
+        cast_v(0, 1, S)
+        tanh_gate(0)
+        weigh(3, 0, 2)
+        weigh(3, 2, 4)
+        quant_q(1, 2, 4)
+        quant_w(3, 0, G)
+        scores(5)
+        exps(5)
+        tanh_gate(1)
+        cast_v(1, 0, S)
+        weigh(4, 0, 2)
+        quant_v(0)
+        values(0)
+        values(1)
+        weigh(4, 2, 4)
+        invert(0)
+        invert(1)
+        quant_w(4, 0, G)
+        make_gate(0, V)
+        scores(6)
+        values(2)
+        values(3)
+        exps(6)
+        tanh_gate(2)
+        tanh_gate(3)
+        weigh(5, 0, 2)
+        finish_early(0)
+        make_gate(1, V)
+        weigh(5, 2, 4)
+        finish_early(1)
+        quant_w(5, 0, G)
+        invert(2)
+        invert(3)
+        make_gate(2, S)
+        scores(7)
+        exps(7)
+        cast_v(1, 1, S)
+        weigh(6, 0, 2)
+        weigh(6, 2, 4)
+        make_gate(3, V)
+        quant_w(6, 0, G)
+        finish_early(2)
+        finish_early(3)
+        weigh(7, 0, 2)
+        quant_v(1)
+        quant_w(7, 0, 2)
+        sigmoid_gate(0)
+        sigmoid_gate(1)
+        sigmoid_gate(2)
+        sigmoid_gate(3)
+        [value(u, g) for g in (0, 1) for u in range(4, 8)]
+        weigh(7, 2, 4)
         invert(4)
-        weigh(last, 0, 2)
-        values(6, 0, G)
-        finish_part(4, 0, 4)
-        quant_w(last, 0, 2)
         invert(5)
-        weigh(last, 2, 4)
-        values(last, 0, 2)
-        finish_part(5, 0, 4)
-        quant_w(last, 2, 4)
+        quant_w(7, 2, 4)
+        [value(u, g) for g in (2, 3) for u in range(4, 8)]
+        finish_late(0, 0, 4)
+        finish_late(1, 0, 4)
         invert(6)
-        values(last, 2, 4)
-        finish_part(6, 0, 4)
-        invert(last)
-        finish_part(last, 0, 2)
-        finish_part(last, 2, 4)
+        invert(7)
+        finish_late(2, 0, 4)
+        finish_late(3, 0, 2)
+        finish_late(3, 2, 4)

@@ -21,13 +21,21 @@ SETS = H // G
 QT = 128
 NQT = NQ // QT
 UNITS = SETS * NQT
-DEPTH = 3
-K_SPLIT = 88
+LAST = UNITS - 1
+WIDTH = QT * PACK
+SLABS = 4
+Y_BANKS = 4
+HALF = P // 2
+RUN = 4
+EXP_BUFS = 3
+PARTS = ((0, 1), (1, 2), (2, 4))
+TANH_BLOCKS = 3
+K_SPLIT = 44
 
 
 def tile_rows_a_exp_kb_mask_gate_kernel(tc, qT, kT, t, v, kb, mask, og, out):
     nc = tc.nc
-    S, V = nc.scalar, nc.vector
+    scalar, vector = nc.scalar, nc.vector
     with ExitStack() as ctx:
         sb = ctx.enter_context(tc.tile_pool(name="sb", bufs=1))
         ps = ctx.enter_context(tc.psum_pool(name="ps", bufs=1))
@@ -36,23 +44,24 @@ def tile_rows_a_exp_kb_mask_gate_kernel(tc, qT, kT, t, v, kb, mask, og, out):
         def tiles(name, count, shape, dtype):
             return [sb.tile(shape, dtype, name="%s%d" % (name, i), align_bytes=64) for i in range(count)]
 
-        k_raw = tiles("k_raw", SETS, [P, PACK, N], F32)
-        q_first = sb.tile([P, PACK, QT], F32, name="q_first")
-        q_rest = sb.tile([P, PACK, NQ - QT], F32, name="q_rest")
-        q_late = sb.tile([P, PACK, NQ], F32, name="q_late")
+        def part_tiles(name):
+            return [sb.tile([P, PACK, (c1 - c0) * QT], F32, name="%s%d" % (name, c0)) for c0, c1 in PARTS]
+
+        k0_raw = tiles("k0_raw", 2, [P, PACK, N // 2], F32)
+        k1_raw = sb.tile([P, PACK, N], F32, name="k1_raw")
+        q0_raw = part_tiles("q0_raw")
+        q1_raw = sb.tile([P, PACK, NQ], F32, name="q1_raw")
         v_raw = tiles("v_raw", SETS, [P, G, PACK, D], F32)
-        og_raw = tiles("og_raw", NQT, [P, G, D], F32)
-        og_late = sb.tile([P, G, NQT * D], F32, name="og_late")
-        mask_first = sb.tile([P, PACK, QT], F32, name="mask_first")
-        mask_rest = sb.tile([P, PACK, NQ - QT], F32, name="mask_rest")
-        scaled_first = sb.tile([P, PACK, QT], F32, name="scaled_first")
-        scaled_rest = sb.tile([P, PACK, NQ - QT], F32, name="scaled_rest")
+        og0_raw = tiles("og0_raw", NQT, [P, G, D], F32)
+        og1_raw = tiles("og1_raw", NQT // 2, [P, G, 2 * D], F32)
+        mask_raw = part_tiles("mask_raw")
         kb_raw = sb.tile([P, PACK], F32, name="kb_raw")
         t_raw = sb.tile([P, PACK], F32, name="t_raw")
         kb_exp = sb.tile([P, PACK], F32, name="kb_exp")
         token_factor = sb.tile([P, PACK], F32, name="token_factor")
         factor = sb.tile([P, NQ * PACK], F32, name="factor")
-        k_bf = tiles("k_bf", SETS, [P, N * PACK], BF16)
+        k0_bf = tiles("k0_bf", 2, [P, N * PACK // 2], BF16)
+        k1_bf = sb.tile([P, N * PACK], BF16, name="k1_bf", align_bytes=64)
         q_bf = tiles("q_bf", SETS, [P, NQ * PACK], BF16)
         v_bf = tiles("v_bf", SETS, [P, G * D * PACK], BF16)
         k_codes = tiles("k_codes", SETS, [P, N], U32)
@@ -61,338 +70,351 @@ def tile_rows_a_exp_kb_mask_gate_kernel(tc, qT, kT, t, v, kb, mask, og, out):
         q_scales = tiles("q_scales", SETS, [P, NQ], U8)
         v_codes = tiles("v_codes", SETS, [P, G * D], U32)
         v_scales = tiles("v_scales", SETS, [P, G * D], U8)
-        p_exp = tiles("p_exp", DEPTH, [P, G, QT * PACK], F32)
-        w_bf = tiles("w_bf", 2, [P, G * QT * PACK], BF16)
+        score_exp = tiles("score_exp", EXP_BUFS, [P, G, WIDTH], F32)
+        w_bf = tiles("w_bf", 2, [P, G * WIDTH], BF16)
         w_codes = tiles("w_codes", UNITS, [P, G * QT], U32)
         w_scales = tiles("w_scales", UNITS, [P, G * QT], U8)
-        th = tiles("th", NQT, [P, 4, D], F32)
-        gate = tiles("gate", 2, [P, 4, D], F32)
-        late_gate = tiles("late_gate", G, [P, 4, D], F32)
-        inv = tiles("inv", UNITS, [P, 4], F32)
-        res = tiles("res", UNITS, [P, 4, D], F32)
+        og_tanh = tiles("og_tanh", TANH_BLOCKS, [P, SLABS, D], F32)
+        scaled_gate = tiles("scaled_gate", 2, [P, SLABS, D], F32)
+        og_sigmoid = tiles("og_sigmoid", UNITS - TANH_BLOCKS, [P, SLABS, D], F32)
+        inverse = tiles("inverse", UNITS, [P, SLABS], F32)
+        result = tiles("result", UNITS, [P, SLABS, D], F32)
         score = [ps.tile([P, PACK, QT], F32, name="score%d" % g) for g in range(G)]
-        y_acc = [ps.tile([P, 4, D], F32, name="y_acc%d" % i) for i in range(4)]
-
-        def heads(s):
-            return slice(s * G, (s + 1) * G)
+        y_bank = [ps.tile([P, SLABS, D], F32, name="y_bank%d" % b) for b in range(Y_BANKS)]
 
         def by_feature(x, s):
-            return x[heads(s)].rearrange("h (p j) n -> (h p) j n", j=PACK)
+            return x[s * G : (s + 1) * G].rearrange("h (p j) n -> (h p) j n", j=PACK)
 
-        mask_rows = mask.rearrange("(p j) n -> p j n", j=PACK)
+        def unit_rows(x, c):
+            return x[:G, c * QT : (c + 1) * QT, :].rearrange("h p e -> p h e")
+
+        def pair_rows(x, h0, h1, pair):
+            rows = x[G + h0 : G + h1, pair * 2 * QT : (pair + 1) * 2 * QT, :]
+            return rows.rearrange("h (p b) e -> p h (b e)", b=2)
+
+        def load_part(part):
+            cols = slice(PARTS[part][0] * QT, PARTS[part][1] * QT)
+            nc.sync.dma_start(out=q0_raw[part][:], in_=by_feature(qT, 0)[:, :, cols])
+            nc.sync.dma_start(out=mask_raw[part][:], in_=mask.rearrange("(p j) n -> p j n", j=PACK)[:, :, cols])
 
         def load_v(s):
             nc.sync.dma_start(
                 out=v_raw[s][:].rearrange("p h j e -> p h (j e)"),
-                in_=v[heads(s)].rearrange("h (p j) e -> p h (j e)", j=PACK),
+                in_=v[s * G : (s + 1) * G].rearrange("h (p j) e -> p h (j e)", j=PACK),
             )
 
-        def load_og(c):
-            nc.sync.dma_start(out=og_raw[c][:], in_=og[heads(0), c * QT : (c + 1) * QT, :].rearrange("h p e -> p h e"))
+        def load_og0(c):
+            nc.sync.dma_start(out=og0_raw[c][:], in_=unit_rows(og, c))
 
         def copy(engine, dst, src):
-            if engine is V:
-                nc.vector.tensor_copy(out=dst, in_=src)
+            if engine is vector:
+                vector.tensor_copy(out=dst, in_=src)
             else:
-                nc.scalar.copy(out=dst, in_=src)
+                scalar.copy(out=dst, in_=src)
 
-        def interleave(engine, dst, src):
+        def round_k(engine, dst, src, lo, hi):
             copy(
                 engine,
-                dst.rearrange("p (c i j) -> p c j i", i=4, j=PACK),
-                src.rearrange("p j (c i) -> p c j i", i=4),
+                dst[:].rearrange("p (r m j) -> p m j r", r=PACK, j=PACK)[:, lo:hi],
+                src[:].rearrange("p j (m r) -> p m j r", r=PACK)[:, lo:hi],
             )
 
-        def deal(engine, dst, src, lo, hi):
+        def round_q0(engine, part, lo, hi):
+            first = PARTS[part][0] * QT
             copy(
                 engine,
-                dst[:].rearrange("p (r s j) -> p s j r", r=4, j=PACK)[:, lo:hi],
-                src[:].rearrange("p j (s r) -> p s j r", r=4)[:, lo:hi],
+                q_bf[0][:, (first + lo) * PACK : (first + hi) * PACK].rearrange("p (c i j) -> p c j i", i=RUN, j=PACK),
+                q0_raw[part][:, :, lo:hi].rearrange("p j (c i) -> p c j i", i=RUN),
             )
 
-        def cast_q0(c0, c1, engine):
-            src = q_first[:] if c0 == 0 else q_rest[:, :, (c0 - 1) * QT : (c1 - 1) * QT]
-            interleave(engine, q_bf[0][:, c0 * QT * PACK : c1 * QT * PACK], src)
+        def round_q1(pair):
+            copy(
+                scalar,
+                q_bf[1][:, pair * 2 * WIDTH : (pair + 1) * 2 * WIDTH].rearrange("p (b m j) -> p m j b", b=2, j=PACK),
+                q1_raw[:, :, pair * 2 * QT : (pair + 1) * 2 * QT].rearrange("p j (m b) -> p m j b", b=2),
+            )
 
-        def cast_k1(half, engine):
-            deal(engine, k_bf[1], k_raw[1], half * 64, (half + 1) * 64)
-
-        def cast_q1(half, engine):
-            deal(engine, q_bf[1], q_late, half * 64, (half + 1) * 64)
-
-        def cast_v(s, half, engine):
-            dst = v_bf[s][:].rearrange("p (h c i j) -> p h c j i", h=G, i=4, j=PACK)
-            src = v_raw[s][:].rearrange("p h j (c i) -> p h c j i", i=4)
+        def round_v(engine, s, half):
+            dst = v_bf[s][:].rearrange("p (h c i j) -> p h c j i", h=G, i=RUN, j=PACK)
+            src = v_raw[s][:].rearrange("p h j (c i) -> p h c j i", i=RUN)
             copy(engine, dst[:, 2 * half : 2 * half + 2], src[:, 2 * half : 2 * half + 2])
 
-        def quantize(codes, scales, src, lo, hi):
-            nc.vector.quantize_mx(
-                out=codes[:, lo:hi].bitcast(FP8X4), scales=scales[:, lo:hi], in_=src[:, lo * PACK : hi * PACK]
+        def quantize(codes, scales, rounded):
+            vector.quantize_mx(out=codes.bitcast(FP8X4), scales=scales, in_=rounded)
+
+        def quantize_k0(half):
+            for r in range(PACK):
+                cols = slice(r * P + half * HALF, r * P + (half + 1) * HALF)
+                rounded = k0_bf[half][:, r * HALF * PACK : (r + 1) * HALF * PACK]
+                quantize(k_codes[0][:, cols], k_scales[0][:, cols], rounded)
+
+        def quantize_q(s, c0, c1):
+            cols = slice(c0 * QT, c1 * QT)
+            quantize(q_codes[s][:, cols], q_scales[s][:, cols], q_bf[s][:, c0 * WIDTH : c1 * WIDTH])
+
+        def quantize_v(s):
+            quantize(v_codes[s][:], v_scales[s][:], v_bf[s][:])
+
+        def quantize_w(u, g0=0, g1=G):
+            cols = slice(g0 * QT, g1 * QT)
+            quantize(w_codes[u][:, cols], w_scales[u][:, cols], w_bf[u % 2][:, g0 * WIDTH : g1 * WIDTH])
+
+        def make_factor(part, c):
+            lo = (c - PARTS[part][0]) * QT
+            vector.tensor_tensor(
+                out=factor[:, c * WIDTH : (c + 1) * WIDTH].rearrange("p (n j) -> p n j", j=PACK),
+                in0=mask_raw[part][:, :, lo : lo + QT].rearrange("p j n -> p n j"),
+                in1=token_factor[:].unsqueeze(1).to_broadcast([P, QT, PACK]),
+                op=ALU.mult,
             )
-
-        def quant_q(s, c0, c1):
-            quantize(q_codes[s], q_scales[s], q_bf[s], c0 * QT, c1 * QT)
-
-        def quant_k(s):
-            quantize(k_codes[s], k_scales[s], k_bf[s], 0, N)
-
-        def quant_v(s):
-            quantize(v_codes[s], v_scales[s], v_bf[s], 0, G * D)
-
-        def scale_mask(c0, c1, engine):
-            cols = slice((c0 - 1) * QT, (c1 - 1) * QT)
-            scaled, raw = (scaled_first, mask_first) if c0 == 0 else (scaled_rest[:, :, cols], mask_rest[:, :, cols])
-            for j in range(PACK):
-                col = token_factor[:, j : j + 1]
-                if engine is V:
-                    nc.vector.tensor_scalar(out=scaled[:, j, :], in0=raw[:, j, :], scalar1=col, scalar2=None, op0=ALU.mult)
-                else:
-                    nc.scalar.activation(out=scaled[:, j, :], in_=raw[:, j, :], func=ACT.Copy, scale=col)
-
-        def make_factor(c0, c1):
-            src = scaled_first[:] if c0 == 0 else scaled_rest[:, :, (c0 - 1) * QT : (c1 - 1) * QT]
-            interleave(V, factor[:, c0 * QT * PACK : c1 * QT * PACK], src)
 
         def scores(u):
             s, c = divmod(u, NQT)
+            queries = slice(c * QT, (c + 1) * QT)
             for g in range(G):
                 rows = slice(g * ROWS, (g + 1) * ROWS)
                 for r in range(PACK):
-                    cols = slice(r * P, (r + 1) * P)
+                    tokens = slice(r * P, (r + 1) * P)
                     nc.tensor.matmul_mx(
                         out=score[g][:, r, :],
-                        lhsT=k_codes[s][rows, cols].bitcast(FP8X4),
-                        lhsT_scale=k_scales[s][rows, cols],
-                        rhs=q_codes[s][rows, c * QT : (c + 1) * QT].bitcast(FP8X4),
-                        rhs_scale=q_scales[s][rows, c * QT : (c + 1) * QT],
+                        lhsT=k_codes[s][rows, tokens].bitcast(FP8X4),
+                        lhsT_scale=k_scales[s][rows, tokens],
+                        rhs=q_codes[s][rows, queries].bitcast(FP8X4),
+                        rhs_scale=q_scales[s][rows, queries],
                         start=True,
                         stop=True,
                     )
 
         def exps(u):
             for g in range(G):
-                nc.scalar.activation(
-                    out=p_exp[u % DEPTH][:, g, :].rearrange("p (n r) -> p n r", r=PACK),
+                scalar.activation(
+                    out=score_exp[u % EXP_BUFS][:, g, :].rearrange("p (n r) -> p n r", r=PACK),
                     in_=score[g][:].rearrange("p r n -> p n r"),
                     func=ACT.Exp,
                 )
 
         def weigh(u, g0, g1):
             s, c = divmod(u, NQT)
-            width = QT * PACK
             if s == 0:
                 unit_factor = factor[:].rearrange("p (c n j) -> p c n j", c=NQT, j=PACK)[:, c]
             else:
-                unit_factor = factor[:].rearrange("p (n c j) -> p c n j", c=NQT, j=PACK)[:, c]
-            nc.vector.tensor_tensor(
-                out=w_bf[u % 2][:, g0 * width : g1 * width].rearrange("p (g n j) -> p g n j", n=QT, j=PACK),
-                in0=p_exp[u % DEPTH][:, g0:g1, :].rearrange("p g (n j) -> p g n j", j=PACK),
+                unit_factor = factor[:].rearrange("p (a n b j) -> p a b n j", a=2, b=2, j=PACK)[:, c // 2, c % 2]
+            vector.tensor_tensor(
+                out=w_bf[u % 2][:, g0 * WIDTH : g1 * WIDTH].rearrange("p (g n j) -> p g n j", n=QT, j=PACK),
+                in0=score_exp[u % EXP_BUFS][:, g0:g1, :].rearrange("p g (n j) -> p g n j", j=PACK),
                 in1=unit_factor.unsqueeze(1).to_broadcast([P, g1 - g0, QT, PACK]),
                 op=ALU.mult,
             )
 
-        def quant_w(u, g0, g1):
-            quantize(w_codes[u], w_scales[u], w_bf[u % 2], g0 * QT, g1 * QT)
-
-        def value(u, g):
+        def values(u, g0=0, g1=G):
             s, c = divmod(u, NQT)
-            cols = slice(g * QT, (g + 1) * QT)
-            nc.tensor.matmul_mx(
-                out=y_acc[c][:, g, :] if s == 0 else y_acc[g][:, c, :],
-                lhsT=w_codes[u][:, cols].bitcast(FP8X4),
-                lhsT_scale=w_scales[u][:, cols],
-                rhs=v_codes[s][:, g * D : (g + 1) * D].bitcast(FP8X4),
-                rhs_scale=v_scales[s][:, g * D : (g + 1) * D],
-                start=True,
-                stop=True,
-            )
-
-        def values(u):
-            for g in range(G):
-                value(u, g)
-
-        def tanh_gate(c):
-            nc.scalar.activation(out=th[c][:], in_=og_raw[c][:], func=ACT.Tanh, scale=0.5)
-
-        def invert(b):
-            nc.vector.reciprocal(out=inv[b][:], in_=y_acc[b % 4][:, :, D - 1])
-
-        def make_gate(c, engine):
-            for g in range(G):
-                col = inv[c][:, g : g + 1]
-                if engine is S:
-                    nc.scalar.activation(
-                        out=gate[c % 2][:, g, :], in_=th[c][:, g, :], func=ACT.Identity, scale=col, bias=col
-                    )
-                    continue
-                nc.vector.tensor_scalar(
-                    out=gate[c % 2][:, g, :], in0=th[c][:, g, :], scalar1=col, scalar2=col, op0=ALU.mult, op1=ALU.add
+            for g in range(g0, g1):
+                bank, slab = (c, g) if s == 0 else (2 * (c // 2) + g // 2, 2 * (g % 2) + c % 2)
+                queries = slice(g * QT, (g + 1) * QT)
+                features = slice(g * D, (g + 1) * D)
+                nc.tensor.matmul_mx(
+                    out=y_bank[bank][:, slab, :],
+                    lhsT=w_codes[u][:, queries].bitcast(FP8X4),
+                    lhsT_scale=w_scales[u][:, queries],
+                    rhs=v_codes[s][:, features].bitcast(FP8X4),
+                    rhs_scale=v_scales[s][:, features],
+                    start=True,
+                    stop=True,
                 )
 
-        def finish_early(c):
-            nc.vector.scalar_tensor_tensor(
-                out=res[c][:].rearrange("p g e -> p (g e)"),
-                in0=y_acc[c][:].rearrange("p g e -> p (g e)"),
+        def invert(b):
+            vector.reciprocal(out=inverse[b][:], in_=y_bank[b % Y_BANKS][:, :, D - 1])
+
+        def store(b, lo, hi):
+            if b < NQT:
+                nc.sync.dma_start(out=unit_rows(out, b), in_=result[b][:])
+            else:
+                pair, first = (b - NQT) // 2, 2 * (b % 2)
+                nc.sync.dma_start(
+                    out=pair_rows(out, first + lo // 2, first + hi // 2, pair),
+                    in_=result[b][:, lo:hi, :].rearrange("p (h b) e -> p h (b e)", b=2),
+                )
+
+        def take_tanh(b):
+            scalar.activation(out=og_tanh[b][:], in_=og0_raw[b][:], func=ACT.Tanh, scale=0.5)
+
+        def scale_gate(b):
+            for slab in range(SLABS):
+                col = inverse[b][:, slab : slab + 1]
+                vector.tensor_scalar(
+                    out=scaled_gate[b % 2][:, slab, :],
+                    in0=og_tanh[b][:, slab, :],
+                    scalar1=col,
+                    scalar2=col,
+                    op0=ALU.mult,
+                    op1=ALU.add,
+                )
+
+        def finish_tanh(b):
+            vector.scalar_tensor_tensor(
+                out=result[b][:].rearrange("p g e -> p (g e)"),
+                in0=y_bank[b][:].rearrange("p g e -> p (g e)"),
                 scalar=0.5,
-                in1=gate[c % 2][:].rearrange("p g e -> p (g e)"),
+                in1=scaled_gate[b % 2][:].rearrange("p g e -> p (g e)"),
                 op0=ALU.mult,
                 op1=ALU.mult,
             )
-            nc.sync.dma_start(out=out[heads(0), c * QT : (c + 1) * QT, :].rearrange("h p e -> p h e"), in_=res[c][:])
+            store(b, 0, SLABS)
 
-        def sigmoid_early(c):
-            nc.scalar.activation(out=th[c][:], in_=og_raw[c][:], func=ACT.Sigmoid)
+        def take_sigmoid(b):
+            gate = og_sigmoid[b - TANH_BLOCKS]
+            if b < NQT:
+                scalar.activation(out=gate[:], in_=og0_raw[b][:], func=ACT.Sigmoid)
+            else:
+                pair, first = (b - NQT) // 2, 2 * (b % 2)
+                scalar.activation(
+                    out=gate[:].rearrange("p (h b) e -> p h (b e)", b=2),
+                    in_=og1_raw[pair][:, first : first + 2, :],
+                    func=ACT.Sigmoid,
+                )
 
-        def finish_mid(c):
-            for g in range(G):
-                nc.vector.scalar_tensor_tensor(
-                    out=res[c][:, g, :],
-                    in0=y_acc[c][:, g, :],
-                    scalar=inv[c][:, g : g + 1],
-                    in1=th[c][:, g, :],
+        def finish_sigmoid(b, lo=0, hi=SLABS):
+            for slab in range(lo, hi):
+                vector.scalar_tensor_tensor(
+                    out=result[b][:, slab, :],
+                    in0=y_bank[b % Y_BANKS][:, slab, :],
+                    scalar=inverse[b][:, slab : slab + 1],
+                    in1=og_sigmoid[b - TANH_BLOCKS][:, slab, :],
                     op0=ALU.mult,
                     op1=ALU.mult,
                 )
-            nc.sync.dma_start(out=out[heads(0), c * QT : (c + 1) * QT, :].rearrange("h p e -> p h e"), in_=res[c][:])
+            store(b, lo, hi)
 
-        def sigmoid_gate(g):
-            nc.scalar.activation(out=late_gate[g][:].rearrange("p c e -> p (c e)"), in_=og_late[:, g, :], func=ACT.Sigmoid)
-
-        def finish_late(g, c0, c1):
-            for c in range(c0, c1):
-                nc.vector.scalar_tensor_tensor(
-                    out=res[NQT + g][:, c, :],
-                    in0=y_acc[g][:, c, :],
-                    scalar=inv[NQT + g][:, c : c + 1],
-                    in1=late_gate[g][:, c, :],
-                    op0=ALU.mult,
-                    op1=ALU.mult,
-                )
-            nc.sync.dma_start(
-                out=out[G + g].rearrange("(p c) e -> p c e", c=NQT)[:, c0:c1, :], in_=res[NQT + g][:, c0:c1, :]
-            )
-
-        nc.scalar.dma_start(out=kb_raw[:], in_=kb.rearrange("(p j) o -> p (j o)", j=PACK))
-        nc.scalar.dma_start(out=t_raw[:], in_=t.rearrange("(p j) o -> p (j o)", j=PACK))
-        nc.sync.dma_start(out=k_raw[0][:], in_=by_feature(kT, 0))
-        nc.sync.dma_start(out=q_first[:], in_=by_feature(qT, 0)[:, :, :QT])
-        nc.sync.dma_start(out=mask_first[:], in_=mask_rows[:, :, :QT])
-        nc.sync.dma_start(out=q_rest[:], in_=by_feature(qT, 0)[:, :, QT:])
-        nc.sync.dma_start(out=mask_rest[:], in_=mask_rows[:, :, QT:])
-        nc.sync.dma_start(out=k_raw[1][:], in_=by_feature(kT, 1))
-        nc.sync.dma_start(out=q_late[:], in_=by_feature(qT, 1))
+        scalar.dma_start(out=kb_raw[:], in_=kb.rearrange("(p j) o -> p (j o)", j=PACK))
+        scalar.dma_start(out=t_raw[:], in_=t.rearrange("(p j) o -> p (j o)", j=PACK))
+        for half in range(2):
+            nc.sync.dma_start(out=k0_raw[half][:], in_=by_feature(kT, 0)[:, :, half * N // 2 : (half + 1) * N // 2])
+        for part in range(len(PARTS)):
+            load_part(part)
+        nc.sync.dma_start(out=k1_raw[:], in_=by_feature(kT, 1))
         load_v(0)
-        load_og(0)
-        load_og(1)
+        nc.sync.dma_start(out=q1_raw[:], in_=by_feature(qT, 1))
+        load_og0(0)
+        load_og0(1)
         load_v(1)
-        load_og(2)
-        load_og(3)
-        nc.sync.dma_start(out=og_late[:], in_=og[heads(1)].rearrange("h (p c) e -> p h (c e)", c=NQT))
+        load_og0(2)
+        load_og0(3)
+        for pair in range(NQT // 2):
+            nc.sync.dma_start(out=og1_raw[pair][:], in_=pair_rows(og, 0, G, pair))
 
-        nc.scalar.activation(out=kb_exp[:], in_=kb_raw[:], func=ACT.Exp)
-        nc.vector.tensor_tensor(out=token_factor[:], in0=kb_exp[:], in1=t_raw[:], op=ALU.mult)
-        deal(V, k_bf[0], k_raw[0], 0, K_SPLIT)
-        deal(S, k_bf[0], k_raw[0], K_SPLIT, P)
-        cast_q0(0, 1, S)
-        quant_k(0)
-        quant_q(0, 0, 1)
-        scale_mask(0, 1, V)
+        scalar.activation(out=kb_exp[:], in_=kb_raw[:], func=ACT.Exp)
+        round_k(vector, k0_bf[0], k0_raw[0], 0, HALF)
+        vector.tensor_tensor(out=token_factor[:], in0=kb_exp[:], in1=t_raw[:], op=ALU.mult)
+        quantize_k0(0)
+        round_k(vector, k0_bf[1], k0_raw[1], 0, K_SPLIT)
+        round_k(scalar, k0_bf[1], k0_raw[1], K_SPLIT, HALF)
+        round_q0(scalar, 0, 0, QT // 2)
+        round_q0(vector, 0, QT // 2, QT)
+        quantize_k0(1)
+        quantize_q(0, 0, 1)
         scores(0)
         exps(0)
-        make_factor(0, 1)
-        cast_q0(1, 2, V)
+        make_factor(0, 0)
+        round_q0(vector, 1, 0, QT)
+        make_factor(1, 1)
+        quantize_q(0, 1, 2)
+
+        def ahead(u):
+            scores(u + 1)
+            exps(u + 1)
+
+        def weigh_halves(u):
+            weigh(u, 0, G // 2)
+            weigh(u, G // 2, G)
+
+        ahead(0)
+        round_k(scalar, k1_bf, k1_raw, 0, HALF)
         weigh(0, 0, 1)
-        quant_q(0, 1, 2)
-        scores(1)
-        exps(1)
-        cast_k1(0, S)
         weigh(0, 1, 2)
-        cast_q0(2, 4, V)
+        round_q0(vector, 2, 0, 2 * QT)
         weigh(0, 2, 3)
-        quant_q(0, 2, 4)
-        scale_mask(1, 4, V)
+        quantize_q(0, 2, 4)
         weigh(0, 3, 4)
-        make_factor(1, 4)
-        quant_w(0, 0, G)
-        scores(2)
-        exps(2)
-        cast_k1(1, S)
-        cast_q1(0, S)
-        weigh(1, 0, 2)
-        weigh(1, 2, 4)
-        cast_q1(1, V)
-        quant_w(1, 0, G)
-        scores(3)
-        exps(3)
-        cast_v(0, 0, S)
-        weigh(2, 0, 2)
-        quant_k(1)
-        quant_q(1, 0, 1)
-        weigh(2, 2, 4)
-        quant_q(1, 1, 2)
-        quant_w(2, 0, G)
-        scores(4)
-        exps(4)
-        cast_v(0, 1, S)
-        tanh_gate(0)
-        weigh(3, 0, 2)
-        weigh(3, 2, 4)
-        quant_q(1, 2, 4)
-        quant_w(3, 0, G)
-        scores(5)
-        exps(5)
-        tanh_gate(1)
-        cast_v(1, 0, S)
-        weigh(4, 0, 2)
-        quant_v(0)
+        make_factor(2, 2)
+        quantize_w(0)
+
+        ahead(1)
+        round_k(scalar, k1_bf, k1_raw, HALF, P)
+        round_q1(0)
+        weigh_halves(1)
+        round_v(vector, 0, 0)
+        quantize_w(1)
+        make_factor(2, 3)
+
+        ahead(2)
+        round_v(scalar, 0, 1)
+        take_tanh(0)
+        weigh_halves(2)
+        quantize(k_codes[1][:], k_scales[1][:], k1_bf[:])
+        quantize_q(1, 0, 2)
+        quantize_w(2)
+
+        ahead(3)
+        round_q1(1)
+        take_tanh(1)
+        weigh_halves(3)
+        quantize_v(0)
         values(0)
         values(1)
-        weigh(4, 2, 4)
-        invert(0)
-        invert(1)
-        quant_w(4, 0, G)
-        make_gate(0, V)
-        scores(6)
+        quantize_w(3)
+
+        scores(5)
         values(2)
         values(3)
-        exps(6)
-        tanh_gate(2)
-        tanh_gate(3)
-        weigh(5, 0, 2)
-        finish_early(0)
-        make_gate(1, V)
-        weigh(5, 2, 4)
-        finish_early(1)
-        quant_w(5, 0, G)
+        exps(5)
+        round_v(scalar, 1, 0)
+        take_tanh(2)
+        weigh(4, 0, 2)
+        invert(0)
+        invert(1)
+        scale_gate(0)
+        weigh(4, 2, 4)
+        finish_tanh(0)
+        quantize_w(4)
+        quantize_q(1, 2, 4)
+        scale_gate(1)
         invert(2)
         invert(3)
-        make_gate(2, S)
-        scores(7)
-        exps(7)
-        cast_v(1, 1, S)
+
+        ahead(5)
+        round_v(scalar, 1, 1)
+        weigh(5, 0, 2)
+        finish_tanh(1)
+        weigh(5, 2, 4)
+        scale_gate(2)
+        quantize_w(5)
+
+        ahead(6)
         weigh(6, 0, 2)
+        finish_tanh(2)
         weigh(6, 2, 4)
-        make_gate(3, V)
-        quant_w(6, 0, G)
-        finish_early(2)
-        finish_early(3)
-        weigh(7, 0, 2)
-        quant_v(1)
-        quant_w(7, 0, 2)
-        sigmoid_gate(0)
-        sigmoid_gate(1)
-        sigmoid_gate(2)
-        sigmoid_gate(3)
-        [value(u, g) for g in (0, 1) for u in range(4, 8)]
-        weigh(7, 2, 4)
+        quantize_v(1)
+        values(4)
+        values(5)
+        quantize_w(6)
+        values(6, 0, 2)
+
+        for b in range(TANH_BLOCKS, UNITS):
+            take_sigmoid(b)
+        weigh(LAST, 0, 2)
         invert(4)
         invert(5)
-        quant_w(7, 2, 4)
-        [value(u, g) for g in (2, 3) for u in range(4, 8)]
-        finish_late(0, 0, 4)
-        finish_late(1, 0, 4)
+        weigh(LAST, 2, 4)
+        quantize_w(LAST, 0, 2)
+        values(LAST, 0, 2)
+        finish_sigmoid(3)
+        quantize_w(LAST, 2, 4)
+        values(6, 2, 4)
+        values(LAST, 2, 4)
+        finish_sigmoid(4)
         invert(6)
+        finish_sigmoid(5)
         invert(7)
-        finish_late(2, 0, 4)
-        finish_late(3, 0, 2)
-        finish_late(3, 2, 4)
+        finish_sigmoid(6)
+        finish_sigmoid(7, 0, 2)
+        finish_sigmoid(7, 2, 4)

from contextlib import ExitStack

import concourse.mybir as mybir

H, D, NQ, N = 8, 128, 512, 512
FLOPS = 2 * 2 * H * NQ * N * D

F32 = mybir.dt.float32
BF16 = mybir.dt.bfloat16
U32 = mybir.dt.uint32
U8 = mybir.dt.uint8
FP8X4 = mybir.dt.float8_e4m3fn_x4
ACT = mybir.ActivationFunctionType
ALU = mybir.AluOpType

P = 128
PACK = 4
ROWS = D // PACK
G = P // ROWS
SETS = H // G
QT = 128
NQT = NQ // QT
UNITS = SETS * NQT
LAST = UNITS - 1
WIDTH = QT * PACK
SLABS = 4
Y_BANKS = 4
HALF = P // 2
RUN = 4
EXP_BUFS = 3
PARTS = ((0, 1), (1, 2), (2, 4))
TANH_BLOCKS = 3
K_SPLIT = 44


def tile_rows_a_exp_kb_mask_gate_kernel(tc, qT, kT, t, v, kb, mask, og, out):
    nc = tc.nc
    scalar, vector = nc.scalar, nc.vector
    with ExitStack() as ctx:
        sb = ctx.enter_context(tc.tile_pool(name="sb", bufs=1))
        ps = ctx.enter_context(tc.psum_pool(name="ps", bufs=1))
        ctx.enter_context(tc.manual_schedule())

        def tiles(name, count, shape, dtype):
            return [sb.tile(shape, dtype, name="%s%d" % (name, i), align_bytes=64) for i in range(count)]

        def part_tiles(name):
            return [sb.tile([P, PACK, (c1 - c0) * QT], F32, name="%s%d" % (name, c0)) for c0, c1 in PARTS]

        k0_raw = tiles("k0_raw", 2, [P, PACK, N // 2], F32)
        k1_raw = sb.tile([P, PACK, N], F32, name="k1_raw")
        q0_raw = part_tiles("q0_raw")
        q1_raw = sb.tile([P, PACK, NQ], F32, name="q1_raw")
        v_raw = tiles("v_raw", SETS, [P, G, PACK, D], F32)
        og0_raw = tiles("og0_raw", NQT, [P, G, D], F32)
        og1_raw = tiles("og1_raw", NQT // 2, [P, G, 2 * D], F32)
        mask_raw = part_tiles("mask_raw")
        kb_raw = sb.tile([P, PACK], F32, name="kb_raw")
        t_raw = sb.tile([P, PACK], F32, name="t_raw")
        kb_exp = sb.tile([P, PACK], F32, name="kb_exp")
        token_factor = sb.tile([P, PACK], F32, name="token_factor")
        factor = sb.tile([P, NQ * PACK], F32, name="factor")
        k0_bf = tiles("k0_bf", 2, [P, N * PACK // 2], BF16)
        k1_bf = sb.tile([P, N * PACK], BF16, name="k1_bf", align_bytes=64)
        q_bf = tiles("q_bf", SETS, [P, NQ * PACK], BF16)
        v_bf = tiles("v_bf", SETS, [P, G * D * PACK], BF16)
        k_codes = tiles("k_codes", SETS, [P, N], U32)
        k_scales = tiles("k_scales", SETS, [P, N], U8)
        q_codes = tiles("q_codes", SETS, [P, NQ], U32)
        q_scales = tiles("q_scales", SETS, [P, NQ], U8)
        v_codes = tiles("v_codes", SETS, [P, G * D], U32)
        v_scales = tiles("v_scales", SETS, [P, G * D], U8)
        score_exp = tiles("score_exp", EXP_BUFS, [P, G, WIDTH], F32)
        w_bf = tiles("w_bf", 2, [P, G * WIDTH], BF16)
        w_codes = tiles("w_codes", UNITS, [P, G * QT], U32)
        w_scales = tiles("w_scales", UNITS, [P, G * QT], U8)
        og_tanh = tiles("og_tanh", TANH_BLOCKS, [P, SLABS, D], F32)
        scaled_gate = tiles("scaled_gate", 2, [P, SLABS, D], F32)
        og_sigmoid = tiles("og_sigmoid", UNITS - TANH_BLOCKS, [P, SLABS, D], F32)
        inverse = tiles("inverse", UNITS, [P, SLABS], F32)
        result = tiles("result", UNITS, [P, SLABS, D], F32)
        score = [ps.tile([P, PACK, QT], F32, name="score%d" % g) for g in range(G)]
        y_bank = [ps.tile([P, SLABS, D], F32, name="y_bank%d" % b) for b in range(Y_BANKS)]

        def by_feature(x, s):
            return x[s * G : (s + 1) * G].rearrange("h (p j) n -> (h p) j n", j=PACK)

        def unit_rows(x, c):
            return x[:G, c * QT : (c + 1) * QT, :].rearrange("h p e -> p h e")

        def pair_rows(x, h0, h1, pair):
            rows = x[G + h0 : G + h1, pair * 2 * QT : (pair + 1) * 2 * QT, :]
            return rows.rearrange("h (p b) e -> p h (b e)", b=2)

        def load_part(part):
            cols = slice(PARTS[part][0] * QT, PARTS[part][1] * QT)
            nc.sync.dma_start(out=q0_raw[part][:], in_=by_feature(qT, 0)[:, :, cols])
            nc.sync.dma_start(out=mask_raw[part][:], in_=mask.rearrange("(p j) n -> p j n", j=PACK)[:, :, cols])

        def load_v(s):
            nc.sync.dma_start(
                out=v_raw[s][:].rearrange("p h j e -> p h (j e)"),
                in_=v[s * G : (s + 1) * G].rearrange("h (p j) e -> p h (j e)", j=PACK),
            )

        def load_og0(c):
            nc.sync.dma_start(out=og0_raw[c][:], in_=unit_rows(og, c))

        def copy(engine, dst, src):
            if engine is vector:
                vector.tensor_copy(out=dst, in_=src)
            else:
                scalar.copy(out=dst, in_=src)

        def round_k(engine, dst, src, lo, hi):
            copy(
                engine,
                dst[:].rearrange("p (r m j) -> p m j r", r=PACK, j=PACK)[:, lo:hi],
                src[:].rearrange("p j (m r) -> p m j r", r=PACK)[:, lo:hi],
            )

        def round_q0(engine, part, lo, hi):
            first = PARTS[part][0] * QT
            copy(
                engine,
                q_bf[0][:, (first + lo) * PACK : (first + hi) * PACK].rearrange("p (c i j) -> p c j i", i=RUN, j=PACK),
                q0_raw[part][:, :, lo:hi].rearrange("p j (c i) -> p c j i", i=RUN),
            )

        def round_q1(pair):
            copy(
                scalar,
                q_bf[1][:, pair * 2 * WIDTH : (pair + 1) * 2 * WIDTH].rearrange("p (b m j) -> p m j b", b=2, j=PACK),
                q1_raw[:, :, pair * 2 * QT : (pair + 1) * 2 * QT].rearrange("p j (m b) -> p m j b", b=2),
            )

        def round_v(engine, s, half):
            dst = v_bf[s][:].rearrange("p (h c i j) -> p h c j i", h=G, i=RUN, j=PACK)
            src = v_raw[s][:].rearrange("p h j (c i) -> p h c j i", i=RUN)
            copy(engine, dst[:, 2 * half : 2 * half + 2], src[:, 2 * half : 2 * half + 2])

        def quantize(codes, scales, rounded):
            vector.quantize_mx(out=codes.bitcast(FP8X4), scales=scales, in_=rounded)

        def quantize_k0(half):
            for r in range(PACK):
                cols = slice(r * P + half * HALF, r * P + (half + 1) * HALF)
                rounded = k0_bf[half][:, r * HALF * PACK : (r + 1) * HALF * PACK]
                quantize(k_codes[0][:, cols], k_scales[0][:, cols], rounded)

        def quantize_q(s, c0, c1):
            cols = slice(c0 * QT, c1 * QT)
            quantize(q_codes[s][:, cols], q_scales[s][:, cols], q_bf[s][:, c0 * WIDTH : c1 * WIDTH])

        def quantize_v(s):
            quantize(v_codes[s][:], v_scales[s][:], v_bf[s][:])

        def quantize_w(u, g0=0, g1=G):
            cols = slice(g0 * QT, g1 * QT)
            quantize(w_codes[u][:, cols], w_scales[u][:, cols], w_bf[u % 2][:, g0 * WIDTH : g1 * WIDTH])

        def make_factor(part, c):
            lo = (c - PARTS[part][0]) * QT
            vector.tensor_tensor(
                out=factor[:, c * WIDTH : (c + 1) * WIDTH].rearrange("p (n j) -> p n j", j=PACK),
                in0=mask_raw[part][:, :, lo : lo + QT].rearrange("p j n -> p n j"),
                in1=token_factor[:].unsqueeze(1).to_broadcast([P, QT, PACK]),
                op=ALU.mult,
            )

        def scores(u):
            s, c = divmod(u, NQT)
            queries = slice(c * QT, (c + 1) * QT)
            for g in range(G):
                rows = slice(g * ROWS, (g + 1) * ROWS)
                for r in range(PACK):
                    tokens = slice(r * P, (r + 1) * P)
                    nc.tensor.matmul_mx(
                        out=score[g][:, r, :],
                        lhsT=k_codes[s][rows, tokens].bitcast(FP8X4),
                        lhsT_scale=k_scales[s][rows, tokens],
                        rhs=q_codes[s][rows, queries].bitcast(FP8X4),
                        rhs_scale=q_scales[s][rows, queries],
                        start=True,
                        stop=True,
                    )

        def exps(u):
            for g in range(G):
                scalar.activation(
                    out=score_exp[u % EXP_BUFS][:, g, :].rearrange("p (n r) -> p n r", r=PACK),
                    in_=score[g][:].rearrange("p r n -> p n r"),
                    func=ACT.Exp,
                )

        def weigh(u, g0, g1):
            s, c = divmod(u, NQT)
            if s == 0:
                unit_factor = factor[:].rearrange("p (c n j) -> p c n j", c=NQT, j=PACK)[:, c]
            else:
                unit_factor = factor[:].rearrange("p (a n b j) -> p a b n j", a=2, b=2, j=PACK)[:, c // 2, c % 2]
            vector.tensor_tensor(
                out=w_bf[u % 2][:, g0 * WIDTH : g1 * WIDTH].rearrange("p (g n j) -> p g n j", n=QT, j=PACK),
                in0=score_exp[u % EXP_BUFS][:, g0:g1, :].rearrange("p g (n j) -> p g n j", j=PACK),
                in1=unit_factor.unsqueeze(1).to_broadcast([P, g1 - g0, QT, PACK]),
                op=ALU.mult,
            )

        def values(u, g0=0, g1=G):
            s, c = divmod(u, NQT)
            for g in range(g0, g1):
                bank, slab = (c, g) if s == 0 else (2 * (c // 2) + g // 2, 2 * (g % 2) + c % 2)
                queries = slice(g * QT, (g + 1) * QT)
                features = slice(g * D, (g + 1) * D)
                nc.tensor.matmul_mx(
                    out=y_bank[bank][:, slab, :],
                    lhsT=w_codes[u][:, queries].bitcast(FP8X4),
                    lhsT_scale=w_scales[u][:, queries],
                    rhs=v_codes[s][:, features].bitcast(FP8X4),
                    rhs_scale=v_scales[s][:, features],
                    start=True,
                    stop=True,
                )

        def invert(b):
            vector.reciprocal(out=inverse[b][:], in_=y_bank[b % Y_BANKS][:, :, D - 1])

        def store(b, lo, hi):
            if b < NQT:
                nc.sync.dma_start(out=unit_rows(out, b), in_=result[b][:])
            else:
                pair, first = (b - NQT) // 2, 2 * (b % 2)
                nc.sync.dma_start(
                    out=pair_rows(out, first + lo // 2, first + hi // 2, pair),
                    in_=result[b][:, lo:hi, :].rearrange("p (h b) e -> p h (b e)", b=2),
                )

        def take_tanh(b):
            scalar.activation(out=og_tanh[b][:], in_=og0_raw[b][:], func=ACT.Tanh, scale=0.5)

        def scale_gate(b):
            for slab in range(SLABS):
                col = inverse[b][:, slab : slab + 1]
                vector.tensor_scalar(
                    out=scaled_gate[b % 2][:, slab, :],
                    in0=og_tanh[b][:, slab, :],
                    scalar1=col,
                    scalar2=col,
                    op0=ALU.mult,
                    op1=ALU.add,
                )

        def finish_tanh(b):
            vector.scalar_tensor_tensor(
                out=result[b][:].rearrange("p g e -> p (g e)"),
                in0=y_bank[b][:].rearrange("p g e -> p (g e)"),
                scalar=0.5,
                in1=scaled_gate[b % 2][:].rearrange("p g e -> p (g e)"),
                op0=ALU.mult,
                op1=ALU.mult,
            )
            store(b, 0, SLABS)

        def take_sigmoid(b):
            gate = og_sigmoid[b - TANH_BLOCKS]
            if b < NQT:
                scalar.activation(out=gate[:], in_=og0_raw[b][:], func=ACT.Sigmoid)
            else:
                pair, first = (b - NQT) // 2, 2 * (b % 2)
                scalar.activation(
                    out=gate[:].rearrange("p (h b) e -> p h (b e)", b=2),
                    in_=og1_raw[pair][:, first : first + 2, :],
                    func=ACT.Sigmoid,
                )

        def finish_sigmoid(b, lo=0, hi=SLABS):
            for slab in range(lo, hi):
                vector.scalar_tensor_tensor(
                    out=result[b][:, slab, :],
                    in0=y_bank[b % Y_BANKS][:, slab, :],
                    scalar=inverse[b][:, slab : slab + 1],
                    in1=og_sigmoid[b - TANH_BLOCKS][:, slab, :],
                    op0=ALU.mult,
                    op1=ALU.mult,
                )
            store(b, lo, hi)

        scalar.dma_start(out=kb_raw[:], in_=kb.rearrange("(p j) o -> p (j o)", j=PACK))
        scalar.dma_start(out=t_raw[:], in_=t.rearrange("(p j) o -> p (j o)", j=PACK))
        for half in range(2):
            nc.sync.dma_start(out=k0_raw[half][:], in_=by_feature(kT, 0)[:, :, half * N // 2 : (half + 1) * N // 2])
        for part in range(len(PARTS)):
            load_part(part)
        nc.sync.dma_start(out=k1_raw[:], in_=by_feature(kT, 1))
        load_v(0)
        nc.sync.dma_start(out=q1_raw[:], in_=by_feature(qT, 1))
        load_og0(0)
        load_og0(1)
        load_v(1)
        load_og0(2)
        load_og0(3)
        for pair in range(NQT // 2):
            nc.sync.dma_start(out=og1_raw[pair][:], in_=pair_rows(og, 0, G, pair))

        scalar.activation(out=kb_exp[:], in_=kb_raw[:], func=ACT.Exp)
        round_k(vector, k0_bf[0], k0_raw[0], 0, HALF)
        vector.tensor_tensor(out=token_factor[:], in0=kb_exp[:], in1=t_raw[:], op=ALU.mult)
        quantize_k0(0)
        round_k(vector, k0_bf[1], k0_raw[1], 0, K_SPLIT)
        round_k(scalar, k0_bf[1], k0_raw[1], K_SPLIT, HALF)
        round_q0(scalar, 0, 0, QT // 2)
        round_q0(vector, 0, QT // 2, QT)
        quantize_k0(1)
        quantize_q(0, 0, 1)
        scores(0)
        exps(0)
        make_factor(0, 0)
        round_q0(vector, 1, 0, QT)
        make_factor(1, 1)
        quantize_q(0, 1, 2)

        def ahead(u):
            scores(u + 1)
            exps(u + 1)

        def weigh_halves(u):
            weigh(u, 0, G // 2)
            weigh(u, G // 2, G)

        ahead(0)
        round_k(scalar, k1_bf, k1_raw, 0, HALF)
        weigh(0, 0, 1)
        weigh(0, 1, 2)
        round_q0(vector, 2, 0, 2 * QT)
        weigh(0, 2, 3)
        quantize_q(0, 2, 4)
        weigh(0, 3, 4)
        make_factor(2, 2)
        quantize_w(0)

        ahead(1)
        round_k(scalar, k1_bf, k1_raw, HALF, P)
        round_q1(0)
        weigh_halves(1)
        round_v(vector, 0, 0)
        quantize_w(1)
        make_factor(2, 3)

        ahead(2)
        round_v(scalar, 0, 1)
        take_tanh(0)
        weigh_halves(2)
        quantize(k_codes[1][:], k_scales[1][:], k1_bf[:])
        quantize_q(1, 0, 2)
        quantize_w(2)

        ahead(3)
        round_q1(1)
        take_tanh(1)
        weigh_halves(3)
        quantize_v(0)
        values(0)
        values(1)
        quantize_w(3)

        scores(5)
        values(2)
        values(3)
        exps(5)
        round_v(scalar, 1, 0)
        take_tanh(2)
        weigh(4, 0, 2)
        invert(0)
        invert(1)
        scale_gate(0)
        weigh(4, 2, 4)
        finish_tanh(0)
        quantize_w(4)
        quantize_q(1, 2, 4)
        scale_gate(1)
        invert(2)
        invert(3)

        ahead(5)
        round_v(scalar, 1, 1)
        weigh(5, 0, 2)
        finish_tanh(1)
        weigh(5, 2, 4)
        scale_gate(2)
        quantize_w(5)

        ahead(6)
        weigh(6, 0, 2)
        finish_tanh(2)
        weigh(6, 2, 4)
        quantize_v(1)
        values(4)
        values(5)
        quantize_w(6)
        values(6, 0, 2)

        for b in range(TANH_BLOCKS, UNITS):
            take_sigmoid(b)
        weigh(LAST, 0, 2)
        invert(4)
        invert(5)
        weigh(LAST, 2, 4)
        quantize_w(LAST, 0, 2)
        values(LAST, 0, 2)
        finish_sigmoid(3)
        quantize_w(LAST, 2, 4)
        values(6, 2, 4)
        values(LAST, 2, 4)
        finish_sigmoid(4)
        invert(6)
        finish_sigmoid(5)
        invert(7)
        finish_sigmoid(6)
        finish_sigmoid(7, 0, 2)
        finish_sigmoid(7, 2, 4)
